import numpy as np
import ml_dtypes


def mxq(x, axis, fmt="e4m3"):
    dtype, down = {"e4m3": (ml_dtypes.float8_e4m3fn, 7), "e5m2": (ml_dtypes.float8_e5m2, 14)}[fmt]
    v = np.moveaxis(np.asarray(x, np.float32).astype(ml_dtypes.bfloat16).astype(np.float64), axis, -1)
    blocks = v.reshape(v.shape[:-1] + (-1, 32))
    amax = np.abs(blocks).max(-1, keepdims=True)
    byte = np.maximum(np.where(amax > 0, np.frexp(amax)[1] - 1 + 127, 0) - down, 1)
    scale = np.exp2(byte - 127.0)
    codes = (blocks / scale).astype(np.float32).astype(dtype).astype(np.float64)
    return np.moveaxis((codes * scale).reshape(v.shape), -1, axis)


WIDE = False


def mx_kscale(k):
    if not WIDE:
        return np.ones(k)
    levels = np.array([10, -10, 5, -5, 0])
    if k % 512:
        return np.exp2(np.random.permutation(np.resize(levels, k // 32))).repeat(32)
    a = np.empty((k // 512, 16))
    for p in range(k // 512):
        a[p, :8] = np.random.permutation(np.resize(levels, 8))
        for g in range(8):
            far = levels[np.abs(levels - a[p, g]) >= 10]
            a[p, g + 8] = far[np.random.randint(len(far))]
    return np.exp2(a.ravel()).repeat(32)


def f64(x):
    return np.asarray(x).astype(np.float64)


def striped8(idx):
    return np.asarray(idx).reshape(8, -1, 16).transpose(0, 2, 1).reshape(128, -1).astype(np.uint16)


def unstriped8(offs):
    return offs.reshape(8, 16, -1).transpose(0, 2, 1).reshape(8, -1).astype(np.int64)


def pick8(x, idx, run):
    r = np.arange(len(x))
    return x[r[:, None], idx[r % (8 * run) // run]]


E2M1 = np.array([0.0, 0.5, 1.0, 1.5, 2.0, 3.0, 4.0, 6.0, -0.0, -0.5, -1.0, -1.5, -2.0, -3.0, -4.0, -6.0])


def pack_weight(w, fmt):
    k, n = w.shape
    w = f64(np.asarray(w, np.float32).astype(ml_dtypes.bfloat16)).reshape(k // 32, 32, n)
    amax = np.abs(w).max(1)
    if fmt == "e4m3":
        byte = np.frexp(amax)[1] - 1 + 127 - 7
    else:
        mant, ex = np.frexp(amax / 6.0)
        byte = np.where(mant > 0.5, ex, ex - 1) + 127
    byte = np.clip(np.where(amax > 0, byte, 1), 1, 254)
    scaled = (w * np.exp2(127.0 - byte)[:, None, :]).reshape(k, n).astype(np.float32)
    by_word = np.ascontiguousarray(scaled.reshape(k // 512, 128, 4, n).transpose(0, 1, 3, 2))
    if fmt == "e4m3":
        words = by_word.astype(ml_dtypes.float8_e4m3fn).view(np.uint8)
    else:
        c = by_word.astype(ml_dtypes.float4_e2m1fn).view(np.uint8) & 0xF
        words = (c[..., 0::2] | (c[..., 1::2] << 4)).reshape(k // 512, 128, 2 * n)
    return np.ascontiguousarray(words), np.ascontiguousarray(byte.astype(np.uint8).reshape(k // 512, 16, n))


def unpack_weight(words, scales, fmt):
    g, _, n = scales.shape
    words = np.ascontiguousarray(words).reshape(g, 128, n, -1)
    if fmt == "e4m3":
        vals = words.view(ml_dtypes.float8_e4m3fn).astype(np.float64)
    else:
        nib = np.empty((g, 128, n, 4), np.uint8)
        nib[..., 0::2] = words & 0xF
        nib[..., 1::2] = words >> 4
        vals = E2M1[nib]
    vals = vals * np.repeat(np.exp2(scales.astype(np.float64) - 127.0), 8, axis=1)[..., None]
    return vals.transpose(0, 1, 3, 2).reshape(g * 512, n)


D, K, T, U, X, I, Q = 512, 512, 1024, 1024, 1024, 512, 128


def setup_inputs():
    n = np.random.standard_normal
    idx = np.stack([np.random.permutation(T)[:I] for _ in range(8)])
    idx2 = np.stack([np.random.permutation(U)[:I] for _ in range(8)])
    idx3 = np.stack([np.random.permutation(U)[:I] for _ in range(8)])
    idx4 = np.stack([np.random.permutation(X)[:I] for _ in range(8)])
    idx5 = np.stack([np.random.permutation(X)[:I] for _ in range(8)])
    idx6 = np.stack([np.random.permutation(T)[:I] for _ in range(8)])
    fd = mx_kscale(D)
    fk = mx_kscale(K)
    wqp = pack_weight(n((D, K)) * 1.0 / np.sqrt(D) * fd[:, None] * fk, "e4m3")
    cachep = pack_weight(n((K, T)) * 1.0 / np.sqrt(K) / fk[:, None], "e2m1")
    draftp = pack_weight(n((K, U)) * 1.0 / np.sqrt(K) / fk[:, None], "e4m3")
    archp = pack_weight(n((D, X)) * 1.0 / np.sqrt(D) * fd[:, None], "e2m1")
    return {
        "states": (n((D, Q)) * 0.95 / fd[:, None]).astype(np.float32),
        "wq_words": wqp[0],
        "wq_scales": wqp[1],
        "cache_words": cachep[0],
        "cache_scales": cachep[1],
        "draft_words": draftp[0],
        "draft_scales": draftp[1],
        "arch_words": archp[0],
        "arch_scales": archp[1],
        "offs": striped8(idx),
        "offs2": striped8(idx2),
        "offs3": striped8(idx3),
        "offs4": striped8(idx4),
        "offs5": striped8(idx5),
        "offs6": striped8(idx6),
    }


def reference(states, wq_words, wq_scales, cache_words, cache_scales, draft_words, draft_scales, arch_words, arch_scales, offs, offs2, offs3, offs4, offs5, offs6):
    idx = unstriped8(offs)
    idx2 = unstriped8(offs2)
    idx3 = unstriped8(offs3)
    idx4 = unstriped8(offs4)
    idx5 = unstriped8(offs5)
    idx6 = unstriped8(offs6)
    wqu = unpack_weight(wq_words, wq_scales, "e4m3")
    cacheu = unpack_weight(cache_words, cache_scales, "e2m1")
    draftu = unpack_weight(draft_words, draft_scales, "e4m3")
    archu = unpack_weight(arch_words, arch_scales, "e2m1")
    statesq = mxq(f64(states), 0, "e4m3")
    qv = wqu.T @ statesq
    qvq = mxq(qv, 0, "e4m3")
    a = qvq.T @ cacheu
    b = qvq.T @ draftu
    c0 = statesq.T @ archu
    f1 = np.zeros((Q, U))
    f1[np.arange(Q)[:, None], idx2[np.arange(Q) % 128 // 16]] = pick8(a, idx, 16)
    f2 = np.zeros((Q, X))
    f2[np.arange(Q)[:, None], idx4[np.arange(Q) % 128 // 16]] = pick8(b, idx3, 16)
    f3 = np.zeros((Q, T))
    f3[np.arange(Q)[:, None], idx6[np.arange(Q) % 128 // 16]] = pick8(c0, idx5, 16)
    aa = a + f3
    bb = b - f1
    cc = np.maximum(c0, f2)
    v = np.maximum(pick8(aa, idx, 16), pick8(bb, idx3, 16))
    y = v - pick8(cc, idx5, 16)
    return y

@@ -1,0 +1,203 @@
+from contextlib import ExitStack
+
+import concourse.mybir as mybir
+
+F32 = mybir.dt.float32
+BF16 = mybir.dt.bfloat16
+I32 = mybir.dt.int32
+U32 = mybir.dt.uint32
+U16 = mybir.dt.uint16
+U8 = mybir.dt.uint8
+FP8X4 = mybir.dt.float8_e4m3fn_x4
+FP4X4 = mybir.dt.float4_e2m1fn_x4
+COPY = mybir.ActivationFunctionType.Copy
+ALU = mybir.AluOpType
+
+P = 128
+PACK = 4
+KDIM = 512
+POOL = 1024
+SLOTS = 512
+HALF = SLOTS // 2
+BANK = 512
+
+FLOPS = 2 * KDIM * P * (KDIM + 3 * POOL)
+
+
+def tile_attend_threecorners_sidethree_kernel(
+    tc, states, wq_words, wq_scales, cache_words, cache_scales, draft_words, draft_scales,
+    arch_words, arch_scales, offs, offs2, offs3, offs4, offs5, offs6, out,
+):
+    nc = tc.nc
+    with ExitStack() as ctx:
+        lists = ctx.enter_context(tc.tile_pool(name="lists", bufs=1))
+        keep = ctx.enter_context(tc.tile_pool(name="keep", bufs=1))
+        psum = ctx.enter_context(tc.psum_pool(name="psum", bufs=1))
+
+        def load_list(src, name):
+            tile = lists.tile([P, SLOTS // 16], U16, name=name)
+            nc.sync.dma_start(tile[:], src)
+            return tile
+
+        def load_scales(src, name):
+            width = src.shape[2]
+            tile = keep.tile([P, width], U8, name=name, align_bytes=64)
+            nc.vector.memset(tile[:].bitcast(I32), 0)
+            rows = src[0].bitcast(I32)
+            for quad in range(4):
+                nc.sync.dma_start(tile[32 * quad : 32 * quad + 4, :].bitcast(I32), rows[4 * quad : 4 * quad + 4, :])
+            return tile
+
+        def load_staged(src, name):
+            width = src.shape[2]
+            stage = keep.tile([4, 4, width // 4], I32, name=name + "_stage")
+            nc.sync.dma_start(stage[:], src[0].bitcast(I32).rearrange("(b r) n -> r b n", b=4))
+            plane = keep.tile([P, width], U8, name=name, align_bytes=64)
+            nc.vector.memset(plane[:].bitcast(I32), 0)
+            return stage, plane
+
+        def spread_staged(stage, plane):
+            for quad in range(4):
+                nc.vector.tensor_copy(plane[32 * quad : 32 * quad + 4, :].bitcast(I32), stage[:, quad, :])
+
+        def load_words(src, name, tag=""):
+            tile = keep.tile([P, src.shape[1]], U8, name=name, tag=tag or name, align_bytes=64)
+            nc.sync.dma_start(tile[:].bitcast(I32), src.bitcast(I32))
+            return tile
+
+        def half(tile, h):
+            return tile[:, h * (HALF // 16) : (h + 1) * (HALF // 16)]
+
+        def cols(h):
+            return slice(h * HALF, (h + 1) * HALF)
+
+        wq_stage, wq_sc = load_staged(wq_scales, "wq_sc")
+        arch_stage, arch_sc = load_staged(arch_scales, "arch_sc")
+        st_raw = keep.tile([P, PACK, P], F32, name="st_raw")
+        nc.sync.dma_start(st_raw[:], states.rearrange("(p t) q -> p t q", t=PACK))
+        wq_raw = load_words(wq_words[0].rearrange("p n t -> p (n t)"), "wq_raw")
+        arch_w = load_words(arch_words[0], "arch_w")
+        l5 = load_list(offs5, "l5")
+        l6 = load_list(offs6, "l6")
+        l1 = load_list(offs, "l1")
+        l3 = load_list(offs3, "l3")
+        cache_w = load_words(cache_words[0], "cache_w")
+        draft_w = load_words(draft_words[0].rearrange("p n t -> p (n t)"), "draft_w", tag="draft_then_aa")
+        l2 = load_list(offs2, "l2")
+        l4 = load_list(offs4, "l4")
+        cache_sc = load_scales(cache_scales, "cache_sc")
+        draft_sc = load_scales(draft_scales, "draft_sc")
+
+        f3 = keep.tile([P, POOL], F32, name="f3")
+        f1 = keep.tile([P, POOL], F32, name="f1")
+        for window in (f3, f1):
+            nc.vector.memset(window[:], 0.0)
+
+        spread_staged(wq_stage, wq_sc)
+        wq_sc_dealt = keep.tile([P, KDIM], U8, name="wq_sc_dealt", align_bytes=64)
+        nc.vector.tensor_copy(
+            wq_sc_dealt[:].rearrange("p (t m) -> p m t", t=PACK),
+            wq_sc[:].rearrange("p (m t) -> p m t", t=PACK),
+        )
+        spread_staged(arch_stage, arch_sc)
+
+        st_bf = keep.tile([P, P, PACK], BF16, name="st_bf", tag="st_then_f2", align_bytes=64)
+        nc.scalar.copy(st_bf[:], st_raw[:].rearrange("p t q -> p q t"))
+        st_codes = keep.tile([P, P], U32, name="st_codes", align_bytes=64)
+        st_sc = keep.tile([P, P], U8, name="st_sc", align_bytes=64)
+        nc.vector.quantize_mx(st_codes[:].bitcast(FP8X4), st_sc[:], st_bf[:].rearrange("p q t -> p (q t)"))
+
+        f2 = keep.tile([P, POOL], F32, name="f2", tag="st_then_f2", align_bytes=64)
+        nc.vector.memset(f2[:], 0.0)
+
+        wq_dealt = keep.tile([P, KDIM], U32, name="wq_dealt", align_bytes=64)
+        nc.scalar.copy(
+            wq_dealt[:].rearrange("p (t m) -> p m t", t=PACK),
+            wq_raw[:].bitcast(U32).rearrange("p (m t) -> p m t", t=PACK),
+        )
+
+        qv_ps = psum.tile([P, PACK, P], F32, name="qv_ps", tag="qv")
+        for t in range(PACK):
+            nc.tensor.matmul_mx(
+                qv_ps[:, t, :],
+                lhsT=wq_dealt[:, t * P : (t + 1) * P].bitcast(FP8X4),
+                lhsT_scale=wq_sc_dealt[:, t * P : (t + 1) * P],
+                rhs=st_codes[:].bitcast(FP8X4),
+                rhs_scale=st_sc[:],
+                start=True,
+                stop=True,
+            )
+
+        def score(codes, scales, words, plane, fmt, width, name, tags):
+            per_col = words.shape[1] // POOL
+            banks = []
+            for j, tag in enumerate(tags):
+                bank = psum.tile([P, width], F32, name="ps_" + name + tag, tag=tag)
+                nc.tensor.matmul_mx(
+                    bank[:],
+                    lhsT=codes[:].bitcast(FP8X4),
+                    lhsT_scale=scales[:],
+                    rhs=words[:, j * width * per_col : (j + 1) * width * per_col].bitcast(fmt),
+                    rhs_scale=plane[:, j * width : (j + 1) * width],
+                    start=True,
+                    stop=True,
+                )
+                banks.append(bank)
+            return banks
+
+        c_banks = score(st_codes, st_sc, arch_w, arch_sc, FP4X4, 256, "c", ["c0", "c1", "c2", "c3"])
+
+        qv_bf = keep.tile([P, P, PACK], BF16, name="qv_bf", align_bytes=64)
+        nc.vector.tensor_copy(qv_bf[:], qv_ps[:].rearrange("p t q -> p q t"))
+        qv_codes = keep.tile([P, P], U32, name="qv_codes", align_bytes=64)
+        qv_sc = keep.tile([P, P], U8, name="qv_sc", align_bytes=64)
+        nc.vector.quantize_mx(qv_codes[:].bitcast(FP8X4), qv_sc[:], qv_bf[:].rearrange("p q t -> p (q t)"))
+
+        c0 = keep.tile([P, POOL], F32, name="c0")
+        for j in range(3):
+            nc.scalar.copy(c0[:, j * 256 : (j + 1) * 256], c_banks[j][:])
+        nc.vector.tensor_copy(c0[:, 768:POOL], c_banks[3][:])
+        c0_g = keep.tile([P, SLOTS], F32, name="c0_g")
+        nc.vector.tensor_copy(c0_g[:, cols(0)], c0[:].indirect(half(l5, 0)))
+        nc.scalar.activation(c0_g[:, cols(1)], c0[:].indirect(half(l5, 1)), COPY)
+        nc.scalar.activation(f3[:].indirect(l6[:]), c0_g[:], COPY)
+
+        a_banks = score(qv_codes, qv_sc, cache_w, cache_sc, FP4X4, BANK, "a", ["c3", "c2"])
+        a = keep.tile([P, POOL], F32, name="a")
+        for j in range(2):
+            nc.vector.tensor_copy(a[:, j * BANK : (j + 1) * BANK], a_banks[j][:])
+        b_banks = score(qv_codes, qv_sc, draft_w, draft_sc, FP8X4, BANK, "b", ["c3", "c2"])
+        b = keep.tile([P, POOL], F32, name="b")
+        a_g = keep.tile([P, SLOTS], F32, name="a_g")
+        for h in range(2):
+            nc.vector.tensor_copy(b[:, h * BANK : (h + 1) * BANK], b_banks[h][:])
+            nc.vector.tensor_copy(a_g[:, cols(h)], a[:].indirect(half(l1, h)))
+        nc.scalar.activation(f1[:].indirect(l2[:]), a_g[:], COPY)
+
+        b_g = keep.tile([P, SLOTS], F32, name="b_g")
+        aa = keep.tile([P, POOL], F32, name="aa", tag="draft_then_aa", align_bytes=64)
+        nc.vector.tensor_copy(b_g[:, cols(0)], b[:].indirect(half(l3, 0)))
+        nc.vector.tensor_tensor(aa[:], a[:], f3[:], ALU.add)
+        nc.vector.tensor_copy(b_g[:, cols(1)], b[:].indirect(half(l3, 1)))
+        nc.scalar.activation(f2[:].indirect(l4[:]), b_g[:], COPY)
+
+        aa_g = keep.tile([P, SLOTS], F32, name="aa_g", tag="aa_g_then_cc")
+        nc.vector.tensor_copy(aa_g[:], aa[:].indirect(l1[:]))
+        bb = keep.tile([P, POOL], F32, name="bb", tag="draft_then_aa", align_bytes=64)
+        nc.vector.tensor_tensor(bb[:], b[:], f1[:], ALU.subtract)
+        bb_g = keep.tile([P, SLOTS], F32, name="bb_g")
+        v = keep.tile([P, SLOTS], F32, name="v")
+        for h in range(2):
+            nc.vector.tensor_copy(bb_g[:, cols(h)], bb[:].indirect(half(l3, h)))
+        for h in range(2):
+            nc.vector.tensor_tensor(v[:, cols(h)], aa_g[:, cols(h)], bb_g[:, cols(h)], ALU.max)
+
+        cc = keep.tile([P, POOL], F32, name="cc", tag="aa_g_then_cc")
+        nc.vector.tensor_tensor(cc[:], c0[:], f2[:], ALU.max)
+        cc_g = keep.tile([P, SLOTS], F32, name="cc_g")
+        nc.vector.tensor_copy(cc_g[:, cols(0)], cc[:].indirect(half(l5, 0)))
+        nc.scalar.activation(cc_g[:, cols(1)], cc[:].indirect(half(l5, 1)), COPY)
+        res = keep.tile([P, SLOTS], F32, name="res")
+        for h in range(2):
+            nc.vector.tensor_tensor(res[:, cols(h)], v[:, cols(h)], cc_g[:, cols(h)], ALU.subtract)
+            nc.sync.dma_start(out[:, cols(h)], res[:, cols(h)])

@@ -20,6 +20,7 @@ POOL = 1024
 SLOTS = 512
 HALF = SLOTS // 2
 BANK = 512
+DEAL_SPLIT = 48
 
 FLOPS = 2 * KDIM * P * (KDIM + 3 * POOL)
 
@@ -39,14 +40,15 @@ def tile_attend_threecorners_sidethree_kernel(
             nc.sync.dma_start(tile[:], src)
             return tile
 
-        def load_scales(src, name):
-            width = src.shape[2]
-            tile = keep.tile([P, width], U8, name=name, align_bytes=64)
+        def zeroed_plane(src, name):
+            tile = keep.tile([P, src.shape[2]], U8, name=name, align_bytes=64)
             nc.vector.memset(tile[:].bitcast(I32), 0)
+            return tile
+
+        def load_scales(tile, src):
             rows = src[0].bitcast(I32)
             for quad in range(4):
                 nc.sync.dma_start(tile[32 * quad : 32 * quad + 4, :].bitcast(I32), rows[4 * quad : 4 * quad + 4, :])
-            return tile
 
         def load_staged(src, name):
             width = src.shape[2]
@@ -71,50 +73,49 @@ def tile_attend_threecorners_sidethree_kernel(
         def cols(h):
             return slice(h * HALF, (h + 1) * HALF)
 
-        wq_stage, wq_sc = load_staged(wq_scales, "wq_sc")
-        arch_stage, arch_sc = load_staged(arch_scales, "arch_sc")
         st_raw = keep.tile([P, PACK, P], F32, name="st_raw")
-        nc.sync.dma_start(st_raw[:], states.rearrange("(p t) q -> p t q", t=PACK))
+        nc.scalar.dma_start(st_raw[:], states.rearrange("(p t) q -> p t q", t=PACK))
+        arch_sc = zeroed_plane(arch_scales, "arch_sc")
+        wq_stage, wq_sc = load_staged(wq_scales, "wq_sc")
         wq_raw = load_words(wq_words[0].rearrange("p n t -> p (n t)"), "wq_raw")
+        load_scales(arch_sc, arch_scales)
         arch_w = load_words(arch_words[0], "arch_w")
         l5 = load_list(offs5, "l5")
         l6 = load_list(offs6, "l6")
-        l1 = load_list(offs, "l1")
-        l3 = load_list(offs3, "l3")
-        cache_w = load_words(cache_words[0], "cache_w")
+        cache_w = load_words(cache_words[0], "cache_w", tag="cache_then_f1")
+        cache_sc = zeroed_plane(cache_scales, "cache_sc")
+        load_scales(cache_sc, cache_scales)
         draft_w = load_words(draft_words[0].rearrange("p n t -> p (n t)"), "draft_w", tag="draft_then_aa")
+        l1 = load_list(offs, "l1")
+        draft_sc = zeroed_plane(draft_scales, "draft_sc")
+        load_scales(draft_sc, draft_scales)
+        l3 = load_list(offs3, "l3")
         l2 = load_list(offs2, "l2")
         l4 = load_list(offs4, "l4")
-        cache_sc = load_scales(cache_scales, "cache_sc")
-        draft_sc = load_scales(draft_scales, "draft_sc")
 
         f3 = keep.tile([P, POOL], F32, name="f3")
-        f1 = keep.tile([P, POOL], F32, name="f1")
-        for window in (f3, f1):
-            nc.vector.memset(window[:], 0.0)
+        nc.vector.memset(f3[:], 0.0)
 
         spread_staged(wq_stage, wq_sc)
         wq_sc_dealt = keep.tile([P, KDIM], U8, name="wq_sc_dealt", align_bytes=64)
         nc.vector.tensor_copy(
-            wq_sc_dealt[:].rearrange("p (t m) -> p m t", t=PACK),
-            wq_sc[:].rearrange("p (m t) -> p m t", t=PACK),
+            wq_sc_dealt[:].rearrange("p (t m) -> p t m", t=PACK),
+            wq_sc[:].rearrange("p (m t) -> p t m", t=PACK),
         )
-        spread_staged(arch_stage, arch_sc)
 
         st_bf = keep.tile([P, P, PACK], BF16, name="st_bf", tag="st_then_f2", align_bytes=64)
         nc.scalar.copy(st_bf[:], st_raw[:].rearrange("p t q -> p q t"))
+        wq_dealt = keep.tile([P, KDIM], U32, name="wq_dealt", align_bytes=64)
+        dealt_view = wq_dealt[:].rearrange("p (t m) -> p m t", t=PACK)
+        raw_view = wq_raw[:].bitcast(U32).rearrange("p (m t) -> p m t", t=PACK)
+        nc.scalar.copy(dealt_view[:, :DEAL_SPLIT, :], raw_view[:, :DEAL_SPLIT, :])
+        nc.vector.tensor_copy(dealt_view[:, DEAL_SPLIT:, :], raw_view[:, DEAL_SPLIT:, :])
         st_codes = keep.tile([P, P], U32, name="st_codes", align_bytes=64)
         st_sc = keep.tile([P, P], U8, name="st_sc", align_bytes=64)
         nc.vector.quantize_mx(st_codes[:].bitcast(FP8X4), st_sc[:], st_bf[:].rearrange("p q t -> p (q t)"))
 
         f2 = keep.tile([P, POOL], F32, name="f2", tag="st_then_f2", align_bytes=64)
-        nc.vector.memset(f2[:], 0.0)
-
-        wq_dealt = keep.tile([P, KDIM], U32, name="wq_dealt", align_bytes=64)
-        nc.scalar.copy(
-            wq_dealt[:].rearrange("p (t m) -> p m t", t=PACK),
-            wq_raw[:].bitcast(U32).rearrange("p (m t) -> p m t", t=PACK),
-        )
+        nc.gpsimd.memset(f2[:], 0.0)
 
         qv_ps = psum.tile([P, PACK, P], F32, name="qv_ps", tag="qv")
         for t in range(PACK):
@@ -153,16 +154,21 @@ def tile_attend_threecorners_sidethree_kernel(
         qv_sc = keep.tile([P, P], U8, name="qv_sc", align_bytes=64)
         nc.vector.quantize_mx(qv_codes[:].bitcast(FP8X4), qv_sc[:], qv_bf[:].rearrange("p q t -> p (q t)"))
 
-        c0 = keep.tile([P, POOL], F32, name="c0")
-        for j in range(3):
-            nc.scalar.copy(c0[:, j * 256 : (j + 1) * 256], c_banks[j][:])
-        nc.vector.tensor_copy(c0[:, 768:POOL], c_banks[3][:])
+        c0 = keep.tile([P, POOL], F32, name="c0", tag="c0_then_v1")
+        for j in range(4):
+            piece = c0[:, j * 256 : (j + 1) * 256]
+            if j % 2 == 0:
+                nc.scalar.copy(piece, c_banks[j][:])
+            else:
+                nc.vector.tensor_copy(piece, c_banks[j][:])
         c0_g = keep.tile([P, SLOTS], F32, name="c0_g")
         nc.vector.tensor_copy(c0_g[:, cols(0)], c0[:].indirect(half(l5, 0)))
         nc.scalar.activation(c0_g[:, cols(1)], c0[:].indirect(half(l5, 1)), COPY)
         nc.scalar.activation(f3[:].indirect(l6[:]), c0_g[:], COPY)
 
         a_banks = score(qv_codes, qv_sc, cache_w, cache_sc, FP4X4, BANK, "a", ["c3", "c2"])
+        f1 = keep.tile([P, POOL], F32, name="f1", tag="cache_then_f1", align_bytes=64)
+        nc.gpsimd.memset(f1[:], 0.0)
         a = keep.tile([P, POOL], F32, name="a")
         for j in range(2):
             nc.vector.tensor_copy(a[:, j * BANK : (j + 1) * BANK], a_banks[j][:])
@@ -181,23 +187,25 @@ def tile_attend_threecorners_sidethree_kernel(
         nc.vector.tensor_copy(b_g[:, cols(1)], b[:].indirect(half(l3, 1)))
         nc.scalar.activation(f2[:].indirect(l4[:]), b_g[:], COPY)
 
-        aa_g = keep.tile([P, SLOTS], F32, name="aa_g", tag="aa_g_then_cc")
+        aa_g = keep.tile([P, SLOTS], F32, name="aa_g")
         nc.vector.tensor_copy(aa_g[:], aa[:].indirect(l1[:]))
         bb = keep.tile([P, POOL], F32, name="bb", tag="draft_then_aa", align_bytes=64)
         nc.vector.tensor_tensor(bb[:], b[:], f1[:], ALU.subtract)
-        bb_g = keep.tile([P, SLOTS], F32, name="bb_g")
-        v = keep.tile([P, SLOTS], F32, name="v")
-        for h in range(2):
-            nc.vector.tensor_copy(bb_g[:, cols(h)], bb[:].indirect(half(l3, h)))
-        for h in range(2):
-            nc.vector.tensor_tensor(v[:, cols(h)], aa_g[:, cols(h)], bb_g[:, cols(h)], ALU.max)
+        bb_g0 = keep.tile([P, HALF], F32, name="bb_g0", tag="bb_g0_then_cc")
+        bb_g1 = keep.tile([P, HALF], F32, name="bb_g1")
+        nc.vector.tensor_copy(bb_g0[:], bb[:].indirect(half(l3, 0)))
+        nc.scalar.activation(bb_g1[:], bb[:].indirect(half(l3, 1)), COPY)
+        v0 = keep.tile([P, HALF], F32, name="v0")
+        nc.vector.tensor_tensor(v0[:], aa_g[:, cols(0)], bb_g0[:], ALU.max)
 
-        cc = keep.tile([P, POOL], F32, name="cc", tag="aa_g_then_cc")
+        cc = keep.tile([P, POOL], F32, name="cc", tag="bb_g0_then_cc")
         nc.vector.tensor_tensor(cc[:], c0[:], f2[:], ALU.max)
+        v1 = keep.tile([P, HALF], F32, name="v1", tag="c0_then_v1")
+        nc.vector.tensor_tensor(v1[:], aa_g[:, cols(1)], bb_g1[:], ALU.max)
         cc_g = keep.tile([P, SLOTS], F32, name="cc_g")
         nc.vector.tensor_copy(cc_g[:, cols(0)], cc[:].indirect(half(l5, 0)))
         nc.scalar.activation(cc_g[:, cols(1)], cc[:].indirect(half(l5, 1)), COPY)
         res = keep.tile([P, SLOTS], F32, name="res")
-        for h in range(2):
-            nc.vector.tensor_tensor(res[:, cols(h)], v[:, cols(h)], cc_g[:, cols(h)], ALU.subtract)
+        for h, v in ((1, v1), (0, v0)):
+            nc.vector.tensor_tensor(res[:, cols(h)], v[:], cc_g[:, cols(h)], ALU.subtract)
             nc.sync.dma_start(out[:, cols(h)], res[:, cols(h)])

@@ -47,8 +47,8 @@ def tile_attend_threecorners_sidethree_kernel(
 
         def load_scales(tile, src):
             rows = src[0].bitcast(I32)
-            for quad in range(4):
-                nc.sync.dma_start(tile[32 * quad : 32 * quad + 4, :].bitcast(I32), rows[4 * quad : 4 * quad + 4, :])
+            for r in range(4):
+                nc.sync.dma_start(tile[r:P:32, :].bitcast(I32), rows[r:16:4, :])
 
         def load_staged(src, name):
             width = src.shape[2]
@@ -156,11 +156,7 @@ def tile_attend_threecorners_sidethree_kernel(
 
         c0 = keep.tile([P, POOL], F32, name="c0", tag="c0_then_v1")
         for j in range(4):
-            piece = c0[:, j * 256 : (j + 1) * 256]
-            if j % 2 == 0:
-                nc.scalar.copy(piece, c_banks[j][:])
-            else:
-                nc.vector.tensor_copy(piece, c_banks[j][:])
+            nc.scalar.copy(c0[:, j * 256 : (j + 1) * 256], c_banks[j][:])
         c0_g = keep.tile([P, SLOTS], F32, name="c0_g")
         nc.vector.tensor_copy(c0_g[:, cols(0)], c0[:].indirect(half(l5, 0)))
         nc.scalar.activation(c0_g[:, cols(1)], c0[:].indirect(half(l5, 1)), COPY)
@@ -175,16 +171,15 @@ def tile_attend_threecorners_sidethree_kernel(
         b_banks = score(qv_codes, qv_sc, draft_w, draft_sc, FP8X4, BANK, "b", ["c3", "c2"])
         b = keep.tile([P, POOL], F32, name="b")
         a_g = keep.tile([P, SLOTS], F32, name="a_g")
-        for h in range(2):
-            nc.vector.tensor_copy(b[:, h * BANK : (h + 1) * BANK], b_banks[h][:])
-            nc.vector.tensor_copy(a_g[:, cols(h)], a[:].indirect(half(l1, h)))
+        nc.vector.tensor_copy(b[:, 0:BANK], b_banks[0][:])
+        nc.vector.tensor_copy(a_g[:], a[:].indirect(l1[:]))
+        nc.vector.tensor_copy(b[:, BANK:POOL], b_banks[1][:])
         nc.scalar.activation(f1[:].indirect(l2[:]), a_g[:], COPY)
 
         b_g = keep.tile([P, SLOTS], F32, name="b_g")
         aa = keep.tile([P, POOL], F32, name="aa", tag="draft_then_aa", align_bytes=64)
-        nc.vector.tensor_copy(b_g[:, cols(0)], b[:].indirect(half(l3, 0)))
         nc.vector.tensor_tensor(aa[:], a[:], f3[:], ALU.add)
-        nc.vector.tensor_copy(b_g[:, cols(1)], b[:].indirect(half(l3, 1)))
+        nc.vector.tensor_copy(b_g[:], b[:].indirect(l3[:]))
         nc.scalar.activation(f2[:].indirect(l4[:]), b_g[:], COPY)
 
         aa_g = keep.tile([P, SLOTS], F32, name="aa_g")
@@ -206,6 +201,6 @@ def tile_attend_threecorners_sidethree_kernel(
         nc.vector.tensor_copy(cc_g[:, cols(0)], cc[:].indirect(half(l5, 0)))
         nc.scalar.activation(cc_g[:, cols(1)], cc[:].indirect(half(l5, 1)), COPY)
         res = keep.tile([P, SLOTS], F32, name="res")
-        for h, v in ((1, v1), (0, v0)):
+        for h, v in enumerate((v0, v1)):
             nc.vector.tensor_tensor(res[:, cols(h)], v[:], cc_g[:, cols(h)], ALU.subtract)
             nc.sync.dma_start(out[:, cols(h)], res[:, cols(h)])

@@ -20,7 +20,7 @@ POOL = 1024
 SLOTS = 512
 HALF = SLOTS // 2
 BANK = 512
-DEAL_SPLIT = 48
+DEAL_SPLIT = 64
 
 FLOPS = 2 * KDIM * P * (KDIM + 3 * POOL)
 
@@ -80,9 +80,9 @@ def tile_attend_threecorners_sidethree_kernel(
         wq_raw = load_words(wq_words[0].rearrange("p n t -> p (n t)"), "wq_raw")
         load_scales(arch_sc, arch_scales)
         arch_w = load_words(arch_words[0], "arch_w")
+        cache_w = load_words(cache_words[0], "cache_w", tag="cache_then_f1")
         l5 = load_list(offs5, "l5")
         l6 = load_list(offs6, "l6")
-        cache_w = load_words(cache_words[0], "cache_w", tag="cache_then_f1")
         cache_sc = zeroed_plane(cache_scales, "cache_sc")
         load_scales(cache_sc, cache_scales)
         draft_w = load_words(draft_words[0].rearrange("p n t -> p (n t)"), "draft_w", tag="draft_then_aa")
@@ -201,6 +201,6 @@ def tile_attend_threecorners_sidethree_kernel(
         nc.vector.tensor_copy(cc_g[:, cols(0)], cc[:].indirect(half(l5, 0)))
         nc.scalar.activation(cc_g[:, cols(1)], cc[:].indirect(half(l5, 1)), COPY)
         res = keep.tile([P, SLOTS], F32, name="res")
-        for h, v in enumerate((v0, v1)):
+        for h, v in ((1, v1), (0, v0)):
             nc.vector.tensor_tensor(res[:, cols(h)], v[:], cc_g[:, cols(h)], ALU.subtract)
             nc.sync.dma_start(out[:, cols(h)], res[:, cols(h)])

@@ -129,24 +129,25 @@ def tile_attend_threecorners_sidethree_kernel(
                 stop=True,
             )
 
-        def score(codes, scales, words, plane, fmt, width, name, tags):
+        def score(codes, scales, words, plane, fmt, widths, name, tags):
             per_col = words.shape[1] // POOL
             banks = []
             for j, tag in enumerate(tags):
+                width, lo = widths[j], sum(widths[:j])
                 bank = psum.tile([P, width], F32, name="ps_" + name + tag, tag=tag)
                 nc.tensor.matmul_mx(
                     bank[:],
                     lhsT=codes[:].bitcast(FP8X4),
                     lhsT_scale=scales[:],
-                    rhs=words[:, j * width * per_col : (j + 1) * width * per_col].bitcast(fmt),
-                    rhs_scale=plane[:, j * width : (j + 1) * width],
+                    rhs=words[:, lo * per_col : (lo + width) * per_col].bitcast(fmt),
+                    rhs_scale=plane[:, lo : lo + width],
                     start=True,
                     stop=True,
                 )
                 banks.append(bank)
             return banks
 
-        c_banks = score(st_codes, st_sc, arch_w, arch_sc, FP4X4, 256, "c", ["c0", "c1", "c2", "c3"])
+        c_banks = score(st_codes, st_sc, arch_w, arch_sc, FP4X4, [256, 256, 256, 128, 128], "c", ["c0", "c1", "c2", "c4", "c3"])
 
         qv_bf = keep.tile([P, P, PACK], BF16, name="qv_bf", align_bytes=64)
         nc.vector.tensor_copy(qv_bf[:], qv_ps[:].rearrange("p t q -> p q t"))
@@ -155,20 +156,22 @@ def tile_attend_threecorners_sidethree_kernel(
         nc.vector.quantize_mx(qv_codes[:].bitcast(FP8X4), qv_sc[:], qv_bf[:].rearrange("p q t -> p (q t)"))
 
         c0 = keep.tile([P, POOL], F32, name="c0", tag="c0_then_v1")
-        for j in range(4):
+        for j in range(3):
             nc.scalar.copy(c0[:, j * 256 : (j + 1) * 256], c_banks[j][:])
+        nc.vector.tensor_copy(c0[:, 768:896], c_banks[3][:])
+        nc.scalar.copy(c0[:, 896:1024], c_banks[4][:])
         c0_g = keep.tile([P, SLOTS], F32, name="c0_g")
         nc.vector.tensor_copy(c0_g[:, cols(0)], c0[:].indirect(half(l5, 0)))
         nc.scalar.activation(c0_g[:, cols(1)], c0[:].indirect(half(l5, 1)), COPY)
         nc.scalar.activation(f3[:].indirect(l6[:]), c0_g[:], COPY)
 
-        a_banks = score(qv_codes, qv_sc, cache_w, cache_sc, FP4X4, BANK, "a", ["c3", "c2"])
+        a_banks = score(qv_codes, qv_sc, cache_w, cache_sc, FP4X4, [BANK, BANK], "a", ["c3", "c2"])
         f1 = keep.tile([P, POOL], F32, name="f1", tag="cache_then_f1", align_bytes=64)
         nc.gpsimd.memset(f1[:], 0.0)
         a = keep.tile([P, POOL], F32, name="a")
         for j in range(2):
             nc.vector.tensor_copy(a[:, j * BANK : (j + 1) * BANK], a_banks[j][:])
-        b_banks = score(qv_codes, qv_sc, draft_w, draft_sc, FP8X4, BANK, "b", ["c3", "c2"])
+        b_banks = score(qv_codes, qv_sc, draft_w, draft_sc, FP8X4, [BANK, BANK], "b", ["c3", "c2"])
         b = keep.tile([P, POOL], F32, name="b")
         a_g = keep.tile([P, SLOTS], F32, name="a_g")
         nc.vector.tensor_copy(b[:, 0:BANK], b_banks[0][:])

from contextlib import ExitStack

import concourse.mybir as mybir

F32 = mybir.dt.float32
BF16 = mybir.dt.bfloat16
I32 = mybir.dt.int32
U32 = mybir.dt.uint32
U16 = mybir.dt.uint16
U8 = mybir.dt.uint8
FP8X4 = mybir.dt.float8_e4m3fn_x4
FP4X4 = mybir.dt.float4_e2m1fn_x4
COPY = mybir.ActivationFunctionType.Copy
ALU = mybir.AluOpType

P = 128
PACK = 4
KDIM = 512
POOL = 1024
SLOTS = 512
HALF = SLOTS // 2
BANK = 512
DEAL_SPLIT = 64

FLOPS = 2 * KDIM * P * (KDIM + 3 * POOL)


def tile_attend_threecorners_sidethree_kernel(
    tc, states, wq_words, wq_scales, cache_words, cache_scales, draft_words, draft_scales,
    arch_words, arch_scales, offs, offs2, offs3, offs4, offs5, offs6, out,
):
    nc = tc.nc
    with ExitStack() as ctx:
        lists = ctx.enter_context(tc.tile_pool(name="lists", bufs=1))
        keep = ctx.enter_context(tc.tile_pool(name="keep", bufs=1))
        psum = ctx.enter_context(tc.psum_pool(name="psum", bufs=1))

        def load_list(src, name):
            tile = lists.tile([P, SLOTS // 16], U16, name=name)
            nc.sync.dma_start(tile[:], src)
            return tile

        def zeroed_plane(src, name):
            tile = keep.tile([P, src.shape[2]], U8, name=name, align_bytes=64)
            nc.vector.memset(tile[:].bitcast(I32), 0)
            return tile

        def load_scales(tile, src):
            rows = src[0].bitcast(I32)
            for r in range(4):
                nc.sync.dma_start(tile[r:P:32, :].bitcast(I32), rows[r:16:4, :])

        def load_staged(src, name):
            width = src.shape[2]
            stage = keep.tile([4, 4, width // 4], I32, name=name + "_stage")
            nc.sync.dma_start(stage[:], src[0].bitcast(I32).rearrange("(b r) n -> r b n", b=4))
            plane = keep.tile([P, width], U8, name=name, align_bytes=64)
            nc.vector.memset(plane[:].bitcast(I32), 0)
            return stage, plane

        def spread_staged(stage, plane):
            for quad in range(4):
                nc.vector.tensor_copy(plane[32 * quad : 32 * quad + 4, :].bitcast(I32), stage[:, quad, :])

        def load_words(src, name, tag=""):
            tile = keep.tile([P, src.shape[1]], U8, name=name, tag=tag or name, align_bytes=64)
            nc.sync.dma_start(tile[:].bitcast(I32), src.bitcast(I32))
            return tile

        def half(tile, h):
            return tile[:, h * (HALF // 16) : (h + 1) * (HALF // 16)]

        def cols(h):
            return slice(h * HALF, (h + 1) * HALF)

        st_raw = keep.tile([P, PACK, P], F32, name="st_raw")
        nc.scalar.dma_start(st_raw[:], states.rearrange("(p t) q -> p t q", t=PACK))
        arch_sc = zeroed_plane(arch_scales, "arch_sc")
        wq_stage, wq_sc = load_staged(wq_scales, "wq_sc")
        wq_raw = load_words(wq_words[0].rearrange("p n t -> p (n t)"), "wq_raw")
        load_scales(arch_sc, arch_scales)
        arch_w = load_words(arch_words[0], "arch_w")
        cache_w = load_words(cache_words[0], "cache_w", tag="cache_then_f1")
        l5 = load_list(offs5, "l5")
        l6 = load_list(offs6, "l6")
        cache_sc = zeroed_plane(cache_scales, "cache_sc")
        load_scales(cache_sc, cache_scales)
        draft_w = load_words(draft_words[0].rearrange("p n t -> p (n t)"), "draft_w", tag="draft_then_aa")
        l1 = load_list(offs, "l1")
        draft_sc = zeroed_plane(draft_scales, "draft_sc")
        load_scales(draft_sc, draft_scales)
        l3 = load_list(offs3, "l3")
        l2 = load_list(offs2, "l2")
        l4 = load_list(offs4, "l4")

        f3 = keep.tile([P, POOL], F32, name="f3")
        nc.vector.memset(f3[:], 0.0)

        spread_staged(wq_stage, wq_sc)
        wq_sc_dealt = keep.tile([P, KDIM], U8, name="wq_sc_dealt", align_bytes=64)
        nc.vector.tensor_copy(
            wq_sc_dealt[:].rearrange("p (t m) -> p t m", t=PACK),
            wq_sc[:].rearrange("p (m t) -> p t m", t=PACK),
        )

        st_bf = keep.tile([P, P, PACK], BF16, name="st_bf", tag="st_then_f2", align_bytes=64)
        nc.scalar.copy(st_bf[:], st_raw[:].rearrange("p t q -> p q t"))
        wq_dealt = keep.tile([P, KDIM], U32, name="wq_dealt", align_bytes=64)
        dealt_view = wq_dealt[:].rearrange("p (t m) -> p m t", t=PACK)
        raw_view = wq_raw[:].bitcast(U32).rearrange("p (m t) -> p m t", t=PACK)
        nc.scalar.copy(dealt_view[:, :DEAL_SPLIT, :], raw_view[:, :DEAL_SPLIT, :])
        nc.vector.tensor_copy(dealt_view[:, DEAL_SPLIT:, :], raw_view[:, DEAL_SPLIT:, :])
        st_codes = keep.tile([P, P], U32, name="st_codes", align_bytes=64)
        st_sc = keep.tile([P, P], U8, name="st_sc", align_bytes=64)
        nc.vector.quantize_mx(st_codes[:].bitcast(FP8X4), st_sc[:], st_bf[:].rearrange("p q t -> p (q t)"))

        f2 = keep.tile([P, POOL], F32, name="f2", tag="st_then_f2", align_bytes=64)
        nc.gpsimd.memset(f2[:], 0.0)

        qv_ps = psum.tile([P, PACK, P], F32, name="qv_ps", tag="qv")
        for t in range(PACK):
            nc.tensor.matmul_mx(
                qv_ps[:, t, :],
                lhsT=wq_dealt[:, t * P : (t + 1) * P].bitcast(FP8X4),
                lhsT_scale=wq_sc_dealt[:, t * P : (t + 1) * P],
                rhs=st_codes[:].bitcast(FP8X4),
                rhs_scale=st_sc[:],
                start=True,
                stop=True,
            )

        def score(codes, scales, words, plane, fmt, widths, name, tags):
            per_col = words.shape[1] // POOL
            banks = []
            for j, tag in enumerate(tags):
                width, lo = widths[j], sum(widths[:j])
                bank = psum.tile([P, width], F32, name="ps_" + name + tag, tag=tag)
                nc.tensor.matmul_mx(
                    bank[:],
                    lhsT=codes[:].bitcast(FP8X4),
                    lhsT_scale=scales[:],
                    rhs=words[:, lo * per_col : (lo + width) * per_col].bitcast(fmt),
                    rhs_scale=plane[:, lo : lo + width],
                    start=True,
                    stop=True,
                )
                banks.append(bank)
            return banks

        c_banks = score(st_codes, st_sc, arch_w, arch_sc, FP4X4, [256, 256, 256, 128, 128], "c", ["c0", "c1", "c2", "c4", "c3"])

        qv_bf = keep.tile([P, P, PACK], BF16, name="qv_bf", align_bytes=64)
        nc.vector.tensor_copy(qv_bf[:], qv_ps[:].rearrange("p t q -> p q t"))
        qv_codes = keep.tile([P, P], U32, name="qv_codes", align_bytes=64)
        qv_sc = keep.tile([P, P], U8, name="qv_sc", align_bytes=64)
        nc.vector.quantize_mx(qv_codes[:].bitcast(FP8X4), qv_sc[:], qv_bf[:].rearrange("p q t -> p (q t)"))

        c0 = keep.tile([P, POOL], F32, name="c0", tag="c0_then_v1")
        for j in range(3):
            nc.scalar.copy(c0[:, j * 256 : (j + 1) * 256], c_banks[j][:])
        nc.vector.tensor_copy(c0[:, 768:896], c_banks[3][:])
        nc.scalar.copy(c0[:, 896:1024], c_banks[4][:])
        c0_g = keep.tile([P, SLOTS], F32, name="c0_g")
        nc.vector.tensor_copy(c0_g[:, cols(0)], c0[:].indirect(half(l5, 0)))
        nc.scalar.activation(c0_g[:, cols(1)], c0[:].indirect(half(l5, 1)), COPY)
        nc.scalar.activation(f3[:].indirect(l6[:]), c0_g[:], COPY)

        a_banks = score(qv_codes, qv_sc, cache_w, cache_sc, FP4X4, [BANK, BANK], "a", ["c3", "c2"])
        f1 = keep.tile([P, POOL], F32, name="f1", tag="cache_then_f1", align_bytes=64)
        nc.gpsimd.memset(f1[:], 0.0)
        a = keep.tile([P, POOL], F32, name="a")
        for j in range(2):
            nc.vector.tensor_copy(a[:, j * BANK : (j + 1) * BANK], a_banks[j][:])
        b_banks = score(qv_codes, qv_sc, draft_w, draft_sc, FP8X4, [BANK, BANK], "b", ["c3", "c2"])
        b = keep.tile([P, POOL], F32, name="b")
        a_g = keep.tile([P, SLOTS], F32, name="a_g")
        nc.vector.tensor_copy(b[:, 0:BANK], b_banks[0][:])
        nc.vector.tensor_copy(a_g[:], a[:].indirect(l1[:]))
        nc.vector.tensor_copy(b[:, BANK:POOL], b_banks[1][:])
        nc.scalar.activation(f1[:].indirect(l2[:]), a_g[:], COPY)

        b_g = keep.tile([P, SLOTS], F32, name="b_g")
        aa = keep.tile([P, POOL], F32, name="aa", tag="draft_then_aa", align_bytes=64)
        nc.vector.tensor_tensor(aa[:], a[:], f3[:], ALU.add)
        nc.vector.tensor_copy(b_g[:], b[:].indirect(l3[:]))
        nc.scalar.activation(f2[:].indirect(l4[:]), b_g[:], COPY)

        aa_g = keep.tile([P, SLOTS], F32, name="aa_g")
        nc.vector.tensor_copy(aa_g[:], aa[:].indirect(l1[:]))
        bb = keep.tile([P, POOL], F32, name="bb", tag="draft_then_aa", align_bytes=64)
        nc.vector.tensor_tensor(bb[:], b[:], f1[:], ALU.subtract)
        bb_g0 = keep.tile([P, HALF], F32, name="bb_g0", tag="bb_g0_then_cc")
        bb_g1 = keep.tile([P, HALF], F32, name="bb_g1")
        nc.vector.tensor_copy(bb_g0[:], bb[:].indirect(half(l3, 0)))
        nc.scalar.activation(bb_g1[:], bb[:].indirect(half(l3, 1)), COPY)
        v0 = keep.tile([P, HALF], F32, name="v0")
        nc.vector.tensor_tensor(v0[:], aa_g[:, cols(0)], bb_g0[:], ALU.max)

        cc = keep.tile([P, POOL], F32, name="cc", tag="bb_g0_then_cc")
        nc.vector.tensor_tensor(cc[:], c0[:], f2[:], ALU.max)
        v1 = keep.tile([P, HALF], F32, name="v1", tag="c0_then_v1")
        nc.vector.tensor_tensor(v1[:], aa_g[:, cols(1)], bb_g1[:], ALU.max)
        cc_g = keep.tile([P, SLOTS], F32, name="cc_g")
        nc.vector.tensor_copy(cc_g[:, cols(0)], cc[:].indirect(half(l5, 0)))
        nc.scalar.activation(cc_g[:, cols(1)], cc[:].indirect(half(l5, 1)), COPY)
        res = keep.tile([P, SLOTS], F32, name="res")
        for h, v in ((1, v1), (0, v0)):
            nc.vector.tensor_tensor(res[:, cols(h)], v[:], cc_g[:, cols(h)], ALU.subtract)
            nc.sync.dma_start(out[:, cols(h)], res[:, cols(h)])
